import numpy as np
import ml_dtypes


def mxq(x, axis, fmt="e4m3"):
    dtype, down = {"e4m3": (ml_dtypes.float8_e4m3fn, 7), "e5m2": (ml_dtypes.float8_e5m2, 14)}[fmt]
    v = np.moveaxis(np.asarray(x, np.float32).astype(ml_dtypes.bfloat16).astype(np.float64), axis, -1)
    blocks = v.reshape(v.shape[:-1] + (-1, 32))
    amax = np.abs(blocks).max(-1, keepdims=True)
    byte = np.maximum(np.where(amax > 0, np.frexp(amax)[1] - 1 + 127, 0) - down, 1)
    scale = np.exp2(byte - 127.0)
    codes = (blocks / scale).astype(np.float32).astype(dtype).astype(np.float64)
    return np.moveaxis((codes * scale).reshape(v.shape), -1, axis)


WIDE = False


def mx_kscale(k):
    if not WIDE:
        return np.ones(k)
    levels = np.array([10, -10, 5, -5, 0])
    if k % 512:
        return np.exp2(np.random.permutation(np.resize(levels, k // 32))).repeat(32)
    a = np.empty((k // 512, 16))
    for p in range(k // 512):
        a[p, :8] = np.random.permutation(np.resize(levels, 8))
        for g in range(8):
            far = levels[np.abs(levels - a[p, g]) >= 10]
            a[p, g + 8] = far[np.random.randint(len(far))]
    return np.exp2(a.ravel()).repeat(32)


def f64(x):
    return np.asarray(x).astype(np.float64)


def striped(idx):
    return np.tile(idx.reshape(-1, 16).T, (8, 1)).astype(np.uint16)


def unstriped(offs):
    return offs[:16].T.reshape(-1).astype(np.int64)


E2M1 = np.array([0.0, 0.5, 1.0, 1.5, 2.0, 3.0, 4.0, 6.0, -0.0, -0.5, -1.0, -1.5, -2.0, -3.0, -4.0, -6.0])


def pack_weight(w, fmt):
    k, n = w.shape
    w = f64(np.asarray(w, np.float32).astype(ml_dtypes.bfloat16)).reshape(k // 32, 32, n)
    amax = np.abs(w).max(1)
    if fmt == "e4m3":
        byte = np.frexp(amax)[1] - 1 + 127 - 7
    else:
        mant, ex = np.frexp(amax / 6.0)
        byte = np.where(mant > 0.5, ex, ex - 1) + 127
    byte = np.clip(np.where(amax > 0, byte, 1), 1, 254)
    scaled = (w * np.exp2(127.0 - byte)[:, None, :]).reshape(k, n).astype(np.float32)
    by_word = np.ascontiguousarray(scaled.reshape(k // 512, 128, 4, n).transpose(0, 1, 3, 2))
    if fmt == "e4m3":
        words = by_word.astype(ml_dtypes.float8_e4m3fn).view(np.uint8)
    else:
        c = by_word.astype(ml_dtypes.float4_e2m1fn).view(np.uint8) & 0xF
        words = (c[..., 0::2] | (c[..., 1::2] << 4)).reshape(k // 512, 128, 2 * n)
    return np.ascontiguousarray(words), np.ascontiguousarray(byte.astype(np.uint8).reshape(k // 512, 16, n))


def unpack_weight(words, scales, fmt):
    g, _, n = scales.shape
    words = np.ascontiguousarray(words).reshape(g, 128, n, -1)
    if fmt == "e4m3":
        vals = words.view(ml_dtypes.float8_e4m3fn).astype(np.float64)
    else:
        nib = np.empty((g, 128, n, 4), np.uint8)
        nib[..., 0::2] = words & 0xF
        nib[..., 1::2] = words >> 4
        vals = E2M1[nib]
    vals = vals * np.repeat(np.exp2(scales.astype(np.float64) - 127.0), 8, axis=1)[..., None]
    return vals.transpose(0, 1, 3, 2).reshape(g * 512, n)


def gelu(v):
    return 0.5 * v * (1.0 + np.tanh(np.sqrt(2.0 / np.pi) * (v + 0.044715 * v**3)))


K, T, S, H, T2, P, N = 1024, 2048, 1024, 1024, 2048, 1024, 512


def setup_inputs():
    n = np.random.standard_normal
    s = mx_kscale(K)[:, None]
    u = mx_kscale(H)[:, None]
    tab_words, tab_scales = pack_weight(n((K, T)) * s, "e4m3")
    w1 = (n((K, H)) / np.sqrt(K) / s * u.T).astype(np.float32)
    w2_words, w2_scales = pack_weight(n((H, N)) / np.sqrt(H) / u, "e2m1")
    return {
        "tab_words": tab_words,
        "tab_scales": tab_scales,
        "offs": striped(np.random.permutation(T)[:S]),
        "w1": w1,
        "page0": (n((H, T2)) * u).astype(np.float32),
        "offs2": striped(np.random.permutation(T2)[:S]),
        "recall": (0.3 + 0.7 * n(H)).astype(np.float32),
        "offs3": striped(np.random.permutation(T2)[:P]),
        "w2_words": w2_words,
        "w2_scales": w2_scales,
        "wind": n((N, P)).astype(np.float32),
    }


def reference(tab_words, tab_scales, offs, w1, page0, offs2, recall, offs3, w2_words, w2_scales, wind):
    v = unpack_weight(tab_words, tab_scales, "e4m3")[:, unstriped(offs)]
    h = mxq(f64(w1), 0, "e4m3").T @ v
    page = f64(page0).copy()
    l2 = unstriped(offs2)
    old = page[:, l2]
    page[:, l2] = np.maximum(old, h) + f64(recall)[:, None] * old
    x = mxq(page[:, unstriped(offs3)], 0, "e4m3")
    w2 = unpack_weight(w2_words, w2_scales, "e2m1")
    y = w2.T @ x
    return np.maximum(y, f64(wind))

@@ -1,0 +1,271 @@
+from contextlib import ExitStack
+
+import concourse.mybir as mybir
+from concourse.masks import make_identity
+
+K, T, S, H, T2, J, N = 1024, 2048, 1024, 1024, 2048, 1024, 512
+FLOPS = 2 * K * H * S + 2 * H * N * J
+
+F32 = mybir.dt.float32
+BF16 = mybir.dt.bfloat16
+I32 = mybir.dt.int32
+U32 = mybir.dt.uint32
+U16 = mybir.dt.uint16
+U8 = mybir.dt.uint8
+E4M3X4 = mybir.dt.float8_e4m3fn_x4
+E2M1X4 = mybir.dt.float4_e2m1fn_x4
+ADD = mybir.AluOpType.add
+MAX = mybir.AluOpType.max
+COPY = mybir.ActivationFunctionType.Copy
+RELU = mybir.ActivationFunctionType.Relu
+
+P = 128
+PACK = 4
+K_PASS = P * PACK
+PASSES = 2
+BANK = 512
+SLICES = PASSES * PACK
+CHUNK = 256
+CHUNKS = J // CHUNK
+
+
+def tile_list_limb_fall_page_kernel(
+    tc, tab_words, tab_scales, offs, w1, page0, offs2, recall, offs3, w2_words, w2_scales, wind, out
+):
+    nc = tc.nc
+    with ExitStack() as ctx:
+        held = ctx.enter_context(tc.tile_pool(name="held", bufs=1))
+        work = ctx.enter_context(tc.tile_pool(name="work", bufs=2))
+        psum = ctx.enter_context(tc.psum_pool(name="psum", bufs=1))
+
+        def bank(k):
+            return psum.tile([P, BANK], F32, name="bank%d" % k, tag="bank%d" % k)
+
+        idx1 = held.tile([P, S // 16], U16, name="idx1")
+        idx2 = held.tile([P, S // 16], U16, name="idx2")
+        idx3 = held.tile([P, J // 16], U16, name="idx3")
+        tab_plane = held.tile([P, T], U8, name="tab_plane", align_bytes=64)
+        w2_plane = held.tile([P, PASSES, N], U8, name="w2_plane", align_bytes=64)
+        ident = held.tile([P, P], F32, name="ident")
+        nc.vector.memset(tab_plane[:].bitcast(I32), 0)
+        nc.vector.memset(w2_plane[:].rearrange("p a n -> p (a n)").bitcast(I32), 0)
+        make_identity(nc, ident[:])
+
+        page_rows = page0.rearrange("(b p t) c -> b t p c", b=PASSES, t=PACK)
+        pages = [held.tile([P, T2], F32, name="page%d" % i) for i in range(SLICES)]
+        tab_w = [held.tile([P, T], I32, name="tab_w%d" % a) for a in range(PASSES)]
+        w1_raw = {}
+
+        def load_page(i):
+            nc.sync.dma_start(pages[i][:], page_rows[i // PACK, i % PACK])
+
+        def load_tab(a):
+            nc.sync.dma_start(tab_w[a][:], tab_words[a].rearrange("p t i -> p (t i)").bitcast(I32))
+
+        def load_w1(a, b):
+            raw = work.tile([P, PACK, K_PASS], F32, name="w1_raw", tag="stage", bufs=4)
+            rows = w1[a * K_PASS : (a + 1) * K_PASS, b * K_PASS : (b + 1) * K_PASS]
+            nc.sync.dma_start(raw[:], rows.rearrange("(p j) c -> p j c", j=PACK))
+            w1_raw[a, b] = raw
+
+        nc.sync.dma_start(idx1[:], offs)
+        for q in range(4):
+            nc.sync.dma_start(
+                tab_plane[32 * q : 32 * q + 4 * PASSES, :].bitcast(I32),
+                tab_scales[:, 4 * q : 4 * q + 4, :].bitcast(I32),
+            )
+        load_tab(0)
+        nc.sync.dma_start(idx2[:], offs2)
+        load_page(0)
+        load_tab(1)
+        load_w1(0, 0)
+        load_w1(1, 0)
+        rec = held.tile([P, PASSES, PACK], F32, name="rec")
+        nc.sync.dma_start(rec[:], recall.rearrange("(b p t) -> p b t", b=PASSES, t=PACK))
+        load_page(1)
+        load_page(2)
+        nc.sync.dma_start(idx3[:], offs3)
+        load_page(3)
+        load_w1(0, 1)
+        load_w1(1, 1)
+        for i in range(4, SLICES):
+            load_page(i)
+        w2_w = held.tile([P, PASSES, 2 * N], U8, name="w2_w", align_bytes=64)
+        nc.sync.dma_start(w2_w[:].bitcast(I32), w2_words.rearrange("a p c -> p a c").bitcast(I32))
+        for q in range(4):
+            nc.sync.dma_start(
+                w2_plane[32 * q : 32 * q + 4, :, :].bitcast(I32),
+                w2_scales[:, 4 * q : 4 * q + 4, :].rearrange("a r n -> r a n").bitcast(I32),
+            )
+        winds = []
+        for pair in range(2):
+            wt = work.tile([P, 2, J], F32, name="wind_t", tag="stage", bufs=4)
+            rows = wind[pair * 2 * P : (pair + 1) * 2 * P, :]
+            nc.sync.dma_start(wt[:], rows.rearrange("(u p) j -> p u j", u=2))
+            winds.append(wt)
+
+        keep = held.tile([P, PASSES, PACK], F32, name="keep")
+        nc.scalar.activation(keep[:], rec[:], COPY, bias=1.0)
+
+        v_plane = held.tile([P, S], U8, name="v_plane", align_bytes=64)
+        v_w = [held.tile([P, S], U32, name="v_w%d" % a, align_bytes=64) for a in range(PASSES)]
+        olds = {}
+
+        def gather_old(i):
+            old = work.tile([P, S], F32, name="old", bufs=3)
+            nc.vector.tensor_copy(old[:], pages[i][:].indirect(idx2[:]))
+            olds[i] = old
+
+        nc.vector.tensor_copy(v_plane[:], tab_plane[:].indirect(idx1[:]))
+        nc.vector.tensor_copy(v_w[0][:], tab_w[0][:].bitcast(U32).indirect(idx1[:]))
+        gather_old(0)
+        nc.vector.tensor_copy(v_w[1][:], tab_w[1][:].bitcast(U32).indirect(idx1[:]))
+
+        w1_q = {}
+
+        def quantize_w1(a, b):
+            grouped = work.tile([P, PACK * K_PASS], BF16, name="w1_grouped", align_bytes=64)
+            nc.scalar.copy(
+                grouped[:].rearrange("p (t m j) -> p m t j", t=PACK, j=PACK),
+                w1_raw[a, b][:].rearrange("p j (m t) -> p m t j", t=PACK),
+            )
+            codes = held.tile([P, K_PASS], U32, name="w1_codes%d%d" % (a, b), align_bytes=64)
+            plane = held.tile([P, K_PASS], U8, name="w1_plane%d%d" % (a, b), align_bytes=64)
+            nc.vector.quantize_mx(codes[:].bitcast(E4M3X4), plane[:], grouped[:])
+            w1_q[a, b] = (codes, plane)
+
+        neg_h = {}
+
+        def make_h(i):
+            b, t = divmod(i, PACK)
+            cols = slice(t * P, (t + 1) * P)
+            for half in range(2):
+                js = slice(half * BANK, (half + 1) * BANK)
+                acc = bank(half)
+                for a in range(PASSES):
+                    codes, plane = w1_q[a, b]
+                    nc.tensor.matmul_mx(
+                        acc[:],
+                        lhsT=codes[:, cols].bitcast(E4M3X4),
+                        lhsT_scale=plane[:, cols],
+                        rhs=v_w[a][:, js].bitcast(E4M3X4),
+                        rhs_scale=v_plane[4 * a : P, js],
+                        start=(a == 0),
+                        stop=(a == PASSES - 1),
+                    )
+                nh = work.tile([P, BANK], F32, name="neg_h", bufs=4)
+                nc.scalar.activation(nh[:], acc[:], COPY, scale=-1.0)
+                neg_h[i, half] = nh
+
+        parts = {}
+
+        def make_parts(i):
+            b, t = divmod(i, PACK)
+            old = olds[i]
+            rise = work.tile([P, S], F32, name="rise")
+            for half in range(2):
+                diff = bank(2 + half)
+                for q in range(4):
+                    blk = slice(q * P, (q + 1) * P)
+                    src = slice(half * BANK + q * P, half * BANK + (q + 1) * P)
+                    nc.tensor.matmul(diff[:, blk], old[:, src], ident[:], start=True, stop=False, is_transpose=True)
+                    nc.tensor.matmul(
+                        diff[:, blk], neg_h[i, half][:, blk], ident[:], start=False, stop=True, is_transpose=True
+                    )
+                rise_t = work.tile([P, BANK], F32, name="rise_t")
+                nc.scalar.activation(rise_t[:], diff[:], RELU, scale=-1.0)
+                back = bank(4 + half)
+                for q in range(4):
+                    blk = slice(q * P, (q + 1) * P)
+                    nc.tensor.transpose(back[:, blk], rise_t[:, blk], ident[:])
+                nc.scalar.copy(rise[:, half * BANK : (half + 1) * BANK], back[:])
+            base = work.tile([P, S], F32, name="base")
+            nc.scalar.activation(base[:], old[:], COPY, scale=keep[:, b, t : t + 1])
+            parts[i] = (rise, base)
+
+        picked = [held.tile([P, PACK, J], BF16, name="picked%d" % b) for b in range(PASSES)]
+
+        def update_and_pick(i):
+            b, t = divmod(i, PACK)
+            rise, base = parts[i]
+            nc.vector.tensor_tensor(pages[i][:].indirect(idx2[:]), rise[:], base[:], ADD)
+            if i < SLICES - 1:
+                nc.vector.tensor_copy(picked[b][:, t, :], pages[i][:].indirect(idx3[:]))
+            else:
+                for c in range(CHUNKS):
+                    nc.vector.tensor_copy(
+                        picked[b][:, t, c * CHUNK : (c + 1) * CHUNK],
+                        pages[i][:].indirect(idx3[:, c * CHUNK // 16 : (c + 1) * CHUNK // 16]),
+                    )
+
+        x_q = {}
+
+        def quantize_x(b, c):
+            grouped = work.tile([P, PACK * CHUNK], BF16, name="x_grouped", bufs=4, align_bytes=64)
+            nc.scalar.copy(
+                grouped[:].rearrange("p (c i t) -> p c t i", i=4, t=PACK),
+                picked[b][:, :, c * CHUNK : (c + 1) * CHUNK].rearrange("p t (c i) -> p c t i", i=4),
+            )
+            codes = held.tile([P, CHUNK], U32, name="x_codes%d%d" % (b, c), align_bytes=64)
+            plane = held.tile([P, CHUNK], U8, name="x_plane%d%d" % (b, c), align_bytes=64)
+            nc.vector.quantize_mx(codes[:].bitcast(E4M3X4), plane[:], grouped[:])
+            x_q[b, c] = (codes, plane)
+
+        y_banks = {}
+        Y_BANK = (6, 0, 2, 4)
+
+        def score_pass(b, c):
+            codes, plane = x_q[b, c]
+            for pair in range(2):
+                if b == 0:
+                    y_banks[c, pair] = bank(Y_BANK[c] + pair)
+                acc = y_banks[c, pair]
+                for u in range(2):
+                    n0 = (2 * pair + u) * P
+                    nc.tensor.matmul_mx(
+                        acc[:, u * CHUNK : (u + 1) * CHUNK],
+                        lhsT=w2_w[:, b, 2 * n0 : 2 * (n0 + P)].bitcast(E2M1X4),
+                        lhsT_scale=w2_plane[:, b, n0 : n0 + P],
+                        rhs=codes[:].bitcast(E4M3X4),
+                        rhs_scale=plane[:],
+                        start=(b == 0 and u == 0),
+                        stop=(b == PASSES - 1 and u == 1),
+                    )
+
+        def finish(c):
+            js = slice(c * CHUNK, (c + 1) * CHUNK)
+            for pair in range(2):
+                res = work.tile([P, 2, CHUNK], F32, name="res", bufs=4)
+                acc = y_banks[c, pair]
+                nc.vector.tensor_tensor(
+                    res[:], acc[:].rearrange("p (u j) -> p u j", u=2), winds[pair][:, :, js], MAX
+                )
+                rows = out[pair * 2 * P : (pair + 1) * 2 * P, js]
+                nc.sync.dma_start(rows.rearrange("(u p) j -> p u j", u=2), res[:])
+
+        quantize_w1(0, 0)
+        quantize_w1(1, 0)
+        make_h(0)
+        gather_old(1)
+        make_parts(0)
+        make_h(1)
+        for i in range(SLICES):
+            if i + 2 < SLICES:
+                gather_old(i + 2)
+            if i + 1 < SLICES:
+                make_parts(i + 1)
+            if i < PASSES:
+                quantize_w1(i, 1)
+            if i + 2 < SLICES:
+                make_h(i + 2)
+            update_and_pick(i)
+            if i >= PACK:
+                quantize_x(0, i - PACK)
+        for c in range(CHUNKS):
+            score_pass(0, c)
+        for c in range(CHUNKS):
+            quantize_x(1, c)
+            score_pass(1, c)
+            if c > 0:
+                finish(c - 1)
+        finish(CHUNKS - 1)

@@ -25,6 +25,9 @@ K_PASS = P * PACK
 PASSES = 2
 BANK = 512
 SLICES = PASSES * PACK
+SLOTS = 5
+CHAIN_PAIR = (0, 0, 1, 2, 2, 0, 1, 3)
+SCORE_PAIR = (0, 1, 3, 0)
 CHUNK = 256
 CHUNKS = J // CHUNK
 
@@ -41,6 +44,12 @@ def tile_list_limb_fall_page_kernel(
         def bank(k):
             return psum.tile([P, BANK], F32, name="bank%d" % k, tag="bank%d" % k)
 
+        def slot(k, shape=(P, S), dtype=F32):
+            return held.tile(list(shape), dtype, name="slot%d" % (k % SLOTS), tag="slot%d" % (k % SLOTS))
+
+        def turned(k, shape, dtype):
+            return held.tile(shape, dtype, name="turned%d" % (k % 4), tag="turned%d" % (k % 4), align_bytes=64)
+
         idx1 = held.tile([P, S // 16], U16, name="idx1")
         idx2 = held.tile([P, S // 16], U16, name="idx2")
         idx3 = held.tile([P, J // 16], U16, name="idx3")
@@ -49,7 +58,6 @@ def tile_list_limb_fall_page_kernel(
         ident = held.tile([P, P], F32, name="ident")
         nc.vector.memset(tab_plane[:].bitcast(I32), 0)
         nc.vector.memset(w2_plane[:].rearrange("p a n -> p (a n)").bitcast(I32), 0)
-        make_identity(nc, ident[:])
 
         page_rows = page0.rearrange("(b p t) c -> b t p c", b=PASSES, t=PACK)
         pages = [held.tile([P, T2], F32, name="page%d" % i) for i in range(SLICES)]
@@ -63,29 +71,32 @@ def tile_list_limb_fall_page_kernel(
             nc.sync.dma_start(tab_w[a][:], tab_words[a].rearrange("p t i -> p (t i)").bitcast(I32))
 
         def load_w1(a, b):
-            raw = work.tile([P, PACK, K_PASS], F32, name="w1_raw", tag="stage", bufs=4)
+            if (a, b) == (1, 0):
+                raw = slot(0, (P, PACK, K_PASS))
+            else:
+                raw = work.tile([P, PACK, K_PASS], F32, name="w1_raw", tag="stage", bufs=3)
             rows = w1[a * K_PASS : (a + 1) * K_PASS, b * K_PASS : (b + 1) * K_PASS]
             nc.sync.dma_start(raw[:], rows.rearrange("(p j) c -> p j c", j=PACK))
             w1_raw[a, b] = raw
 
         nc.sync.dma_start(idx1[:], offs)
+        rec = held.tile([P, PASSES, PACK], F32, name="rec")
+        nc.scalar.dma_start(rec[:], recall.rearrange("(b p t) -> p b t", b=PASSES, t=PACK))
         for q in range(4):
-            nc.sync.dma_start(
+            nc.gpsimd.dma_start(
                 tab_plane[32 * q : 32 * q + 4 * PASSES, :].bitcast(I32),
                 tab_scales[:, 4 * q : 4 * q + 4, :].bitcast(I32),
             )
+        make_identity(nc, ident[:])
         load_tab(0)
         nc.sync.dma_start(idx2[:], offs2)
         load_page(0)
         load_tab(1)
         load_w1(0, 0)
         load_w1(1, 0)
-        rec = held.tile([P, PASSES, PACK], F32, name="rec")
-        nc.sync.dma_start(rec[:], recall.rearrange("(b p t) -> p b t", b=PASSES, t=PACK))
-        load_page(1)
-        load_page(2)
+        for i in range(1, 4):
+            load_page(i)
         nc.sync.dma_start(idx3[:], offs3)
-        load_page(3)
         load_w1(0, 1)
         load_w1(1, 1)
         for i in range(4, SLICES):
@@ -99,126 +110,123 @@ def tile_list_limb_fall_page_kernel(
             )
         winds = []
         for pair in range(2):
-            wt = work.tile([P, 2, J], F32, name="wind_t", tag="stage", bufs=4)
+            wt = work.tile([P, 2, J], F32, name="wind_t", tag="stage", bufs=3)
             rows = wind[pair * 2 * P : (pair + 1) * 2 * P, :]
             nc.sync.dma_start(wt[:], rows.rearrange("(u p) j -> p u j", u=2))
             winds.append(wt)
 
         keep = held.tile([P, PASSES, PACK], F32, name="keep")
-        nc.scalar.activation(keep[:], rec[:], COPY, bias=1.0)
 
         v_plane = held.tile([P, S], U8, name="v_plane", align_bytes=64)
         v_w = [held.tile([P, S], U32, name="v_w%d" % a, align_bytes=64) for a in range(PASSES)]
         olds = {}
 
         def gather_old(i):
-            old = work.tile([P, S], F32, name="old", bufs=3)
+            old = slot(i + 1)
             nc.vector.tensor_copy(old[:], pages[i][:].indirect(idx2[:]))
             olds[i] = old
 
-        nc.vector.tensor_copy(v_plane[:], tab_plane[:].indirect(idx1[:]))
         nc.vector.tensor_copy(v_w[0][:], tab_w[0][:].bitcast(U32).indirect(idx1[:]))
+        nc.vector.tensor_copy(v_plane[:], tab_plane[:].indirect(idx1[:]))
         gather_old(0)
         nc.vector.tensor_copy(v_w[1][:], tab_w[1][:].bitcast(U32).indirect(idx1[:]))
 
         w1_q = {}
 
-        def quantize_w1(a, b):
-            grouped = work.tile([P, PACK * K_PASS], BF16, name="w1_grouped", align_bytes=64)
+        def quantize_w1(a, b, t0, t1, grouped):
+            width = (t1 - t0) * P
             nc.scalar.copy(
-                grouped[:].rearrange("p (t m j) -> p m t j", t=PACK, j=PACK),
-                w1_raw[a, b][:].rearrange("p j (m t) -> p m t j", t=PACK),
+                grouped[:].rearrange("p (t m j) -> p m t j", m=P, j=PACK),
+                w1_raw[a, b][:].rearrange("p j (m t) -> p m t j", t=PACK)[:, :, t0:t1, :],
             )
-            codes = held.tile([P, K_PASS], U32, name="w1_codes%d%d" % (a, b), align_bytes=64)
-            plane = held.tile([P, K_PASS], U8, name="w1_plane%d%d" % (a, b), align_bytes=64)
+            codes = held.tile([P, width], U32, name="w1_codes%d%d%d" % (a, b, t0), align_bytes=64)
+            plane = held.tile([P, width], U8, name="w1_plane%d%d%d" % (a, b, t0), align_bytes=64)
             nc.vector.quantize_mx(codes[:].bitcast(E4M3X4), plane[:], grouped[:])
-            w1_q[a, b] = (codes, plane)
-
-        neg_h = {}
-
-        def make_h(i):
-            b, t = divmod(i, PACK)
-            cols = slice(t * P, (t + 1) * P)
-            for half in range(2):
-                js = slice(half * BANK, (half + 1) * BANK)
-                acc = bank(half)
-                for a in range(PASSES):
-                    codes, plane = w1_q[a, b]
-                    nc.tensor.matmul_mx(
-                        acc[:],
-                        lhsT=codes[:, cols].bitcast(E4M3X4),
-                        lhsT_scale=plane[:, cols],
-                        rhs=v_w[a][:, js].bitcast(E4M3X4),
-                        rhs_scale=v_plane[4 * a : P, js],
-                        start=(a == 0),
-                        stop=(a == PASSES - 1),
-                    )
-                nh = work.tile([P, BANK], F32, name="neg_h", bufs=4)
-                nc.scalar.activation(nh[:], acc[:], COPY, scale=-1.0)
-                neg_h[i, half] = nh
+            for t in range(t0, t1):
+                cols = slice((t - t0) * P, (t - t0 + 1) * P)
+                w1_q[a, b, t] = (codes[:, cols], plane[:, cols])
 
         parts = {}
 
         def make_parts(i):
             b, t = divmod(i, PACK)
             old = olds[i]
+            scratch = slot(i)
+            rise_t = turned(i, [P, S], F32)
             rise = work.tile([P, S], F32, name="rise")
-            for half in range(2):
-                diff = bank(2 + half)
+            halves = [slice(half * BANK, (half + 1) * BANK) for half in range(2)]
+            for half, js in enumerate(halves):
+                acc = bank(2 * CHAIN_PAIR[i] + half)
+                for a in range(PASSES):
+                    codes, plane = w1_q[a, b, t]
+                    nc.tensor.matmul_mx(
+                        acc[:],
+                        lhsT=codes.bitcast(E4M3X4),
+                        lhsT_scale=plane,
+                        rhs=v_w[a][:, js].bitcast(E4M3X4),
+                        rhs_scale=v_plane[4 * a : P, js],
+                        start=(a == 0),
+                        stop=(a == PASSES - 1),
+                    )
+                nc.scalar.activation(scratch[:, js], acc[:], COPY, scale=-1.0)
+            for half, js in enumerate(halves):
+                diff = bank(2 * CHAIN_PAIR[i] + half)
                 for q in range(4):
                     blk = slice(q * P, (q + 1) * P)
                     src = slice(half * BANK + q * P, half * BANK + (q + 1) * P)
-                    nc.tensor.matmul(diff[:, blk], old[:, src], ident[:], start=True, stop=False, is_transpose=True)
-                    nc.tensor.matmul(
-                        diff[:, blk], neg_h[i, half][:, blk], ident[:], start=False, stop=True, is_transpose=True
-                    )
-                rise_t = work.tile([P, BANK], F32, name="rise_t")
-                nc.scalar.activation(rise_t[:], diff[:], RELU, scale=-1.0)
-                back = bank(4 + half)
+                    nc.tensor.matmul(diff[:, blk], scratch[:, src], ident[:], start=True, stop=False, is_transpose=True)
+                    nc.tensor.matmul(diff[:, blk], old[:, src], ident[:], start=False, stop=True, is_transpose=True)
+                nc.scalar.activation(rise_t[:, js], diff[:], RELU, scale=-1.0)
+            for half, js in enumerate(halves):
+                back = bank(2 * CHAIN_PAIR[i] + half)
                 for q in range(4):
-                    blk = slice(q * P, (q + 1) * P)
-                    nc.tensor.transpose(back[:, blk], rise_t[:, blk], ident[:])
-                nc.scalar.copy(rise[:, half * BANK : (half + 1) * BANK], back[:])
-            base = work.tile([P, S], F32, name="base")
-            nc.scalar.activation(base[:], old[:], COPY, scale=keep[:, b, t : t + 1])
-            parts[i] = (rise, base)
+                    src = slice(half * BANK + q * P, half * BANK + (q + 1) * P)
+                    nc.tensor.transpose(back[:, q * P : (q + 1) * P], rise_t[:, src], ident[:])
+                nc.scalar.copy(rise[:, js], back[:])
+            nc.scalar.activation(scratch[:], old[:], COPY, scale=keep[:, b, t : t + 1])
+            parts[i] = (rise, scratch)
 
-        picked = [held.tile([P, PACK, J], BF16, name="picked%d" % b) for b in range(PASSES)]
+        picked = {}
 
-        def update_and_pick(i):
-            b, t = divmod(i, PACK)
+        def update(i):
             rise, base = parts[i]
-            nc.vector.tensor_tensor(pages[i][:].indirect(idx2[:]), rise[:], base[:], ADD)
-            if i < SLICES - 1:
-                nc.vector.tensor_copy(picked[b][:, t, :], pages[i][:].indirect(idx3[:]))
+            if i in (2, 3):
+                nc.vector.tensor_tensor(rise[:], rise[:], base[:], ADD)
+                nc.vector.tensor_copy(pages[i][:].indirect(idx2[:]), rise[:])
             else:
-                for c in range(CHUNKS):
-                    nc.vector.tensor_copy(
-                        picked[b][:, t, c * CHUNK : (c + 1) * CHUNK],
-                        pages[i][:].indirect(idx3[:, c * CHUNK // 16 : (c + 1) * CHUNK // 16]),
-                    )
+                nc.vector.tensor_tensor(pages[i][:].indirect(idx2[:]), rise[:], base[:], ADD)
+
+        def pick(i, tile, j0, c0, c1):
+            nc.vector.tensor_copy(
+                tile[:, i % PACK, c0 * CHUNK - j0 : c1 * CHUNK - j0],
+                pages[i][:].indirect(idx3[:, c0 * CHUNK // 16 : c1 * CHUNK // 16]),
+            )
+            for c in range(c0, c1):
+                picked[i // PACK, c] = (tile, j0)
 
         x_q = {}
 
-        def quantize_x(b, c):
-            grouped = work.tile([P, PACK * CHUNK], BF16, name="x_grouped", bufs=4, align_bytes=64)
+        def quantize_x(b, c0, c1, grouped):
+            width = (c1 - c0) * CHUNK
+            tile, j0 = picked[b, c0]
             nc.scalar.copy(
                 grouped[:].rearrange("p (c i t) -> p c t i", i=4, t=PACK),
-                picked[b][:, :, c * CHUNK : (c + 1) * CHUNK].rearrange("p t (c i) -> p c t i", i=4),
+                tile[:, :, c0 * CHUNK - j0 : c1 * CHUNK - j0].rearrange("p t (c i) -> p c t i", i=4),
             )
-            codes = held.tile([P, CHUNK], U32, name="x_codes%d%d" % (b, c), align_bytes=64)
-            plane = held.tile([P, CHUNK], U8, name="x_plane%d%d" % (b, c), align_bytes=64)
+            codes = held.tile([P, width], U32, name="x_codes%d%d" % (b, c0), align_bytes=64)
+            plane = held.tile([P, width], U8, name="x_plane%d%d" % (b, c0), align_bytes=64)
             nc.vector.quantize_mx(codes[:].bitcast(E4M3X4), plane[:], grouped[:])
-            x_q[b, c] = (codes, plane)
+            for c in range(c0, c1):
+                cols = slice((c - c0) * CHUNK, (c - c0 + 1) * CHUNK)
+                x_q[b, c] = (codes[:, cols], plane[:, cols])
 
         y_banks = {}
-        Y_BANK = (6, 0, 2, 4)
 
         def score_pass(b, c):
             codes, plane = x_q[b, c]
             for pair in range(2):
                 if b == 0:
-                    y_banks[c, pair] = bank(Y_BANK[c] + pair)
+                    y_banks[c, pair] = bank(2 * SCORE_PAIR[c] + pair)
                 acc = y_banks[c, pair]
                 for u in range(2):
                     n0 = (2 * pair + u) * P
@@ -226,8 +234,8 @@ def tile_list_limb_fall_page_kernel(
                         acc[:, u * CHUNK : (u + 1) * CHUNK],
                         lhsT=w2_w[:, b, 2 * n0 : 2 * (n0 + P)].bitcast(E2M1X4),
                         lhsT_scale=w2_plane[:, b, n0 : n0 + P],
-                        rhs=codes[:].bitcast(E4M3X4),
-                        rhs_scale=plane[:],
+                        rhs=codes.bitcast(E4M3X4),
+                        rhs_scale=plane,
                         start=(b == 0 and u == 0),
                         stop=(b == PASSES - 1 and u == 1),
                     )
@@ -243,29 +251,45 @@ def tile_list_limb_fall_page_kernel(
                 rows = out[pair * 2 * P : (pair + 1) * 2 * P, js]
                 nc.sync.dma_start(rows.rearrange("(u p) j -> p u j", u=2), res[:])
 
-        quantize_w1(0, 0)
-        quantize_w1(1, 0)
-        make_h(0)
-        gather_old(1)
+        nc.scalar.activation(keep[:], rec[:], COPY, bias=1.0)
+        for a, t0, t1 in ((0, 0, PACK), (1, 0, 1), (1, 1, PACK)):
+            grouped = held.tile([P, PACK * (t1 - t0) * P], BF16, name="w1_grouped%d%d" % (a, t0), align_bytes=64)
+            quantize_w1(a, 0, t0, t1, grouped)
         make_parts(0)
-        make_h(1)
+        for i in range(1, SLOTS - 1):
+            gather_old(i)
+        first = held.tile([P, PACK, J], BF16, name="first")
+        early = held.tile([P, PACK, J // 2], BF16, name="early")
         for i in range(SLICES):
-            if i + 2 < SLICES:
-                gather_old(i + 2)
             if i + 1 < SLICES:
                 make_parts(i + 1)
+            update(i)
+            if i + SLOTS - 1 < SLICES:
+                gather_old(i + SLOTS - 1)
+            if i < PACK:
+                pick(i, first, 0, 0, CHUNKS)
+            elif i < SLICES - 1:
+                pick(i, early, 0, 0, CHUNKS // 2)
             if i < PASSES:
-                quantize_w1(i, 1)
-            if i + 2 < SLICES:
-                make_h(i + 2)
-            update_and_pick(i)
-            if i >= PACK:
-                quantize_x(0, i - PACK)
-        for c in range(CHUNKS):
+                quantize_w1(i, 1, 0, PACK, turned(i, [P, PACK * K_PASS], BF16))
+            if i in (4, 5):
+                c0 = 2 * (i - 4)
+                quantize_x(0, c0, c0 + 2, turned(i, [P, 2 * PACK * CHUNK], BF16))
+        for c in range(CHUNKS - 1):
             score_pass(0, c)
+        late = slot(SLICES - 1, (P, PACK, J // 2), BF16)
         for c in range(CHUNKS):
-            quantize_x(1, c)
+            if c < CHUNKS // 2:
+                pick(SLICES - 1, early, 0, c, c + 1)
+            if c == CHUNKS // 2:
+                for i in range(PACK, SLICES):
+                    pick(i, late, J // 2, CHUNKS // 2, CHUNKS)
+                finish(0)
+            grouped = work.tile([P, PACK * CHUNK], BF16, name="x_grouped", bufs=4, align_bytes=64)
+            quantize_x(1, c, c + 1, grouped)
+            if c == CHUNKS - 1:
+                score_pass(0, c)
             score_pass(1, c)
-            if c > 0:
+            if c >= CHUNKS // 2:
                 finish(c - 1)
         finish(CHUNKS - 1)

@@ -190,11 +190,7 @@ def tile_list_limb_fall_page_kernel(
 
         def update(i):
             rise, base = parts[i]
-            if i in (2, 3):
-                nc.vector.tensor_tensor(rise[:], rise[:], base[:], ADD)
-                nc.vector.tensor_copy(pages[i][:].indirect(idx2[:]), rise[:])
-            else:
-                nc.vector.tensor_tensor(pages[i][:].indirect(idx2[:]), rise[:], base[:], ADD)
+            nc.vector.tensor_tensor(pages[i][:].indirect(idx2[:]), rise[:], base[:], ADD)
 
         def pick(i, tile, j0, c0, c1):
             nc.vector.tensor_copy(

from contextlib import ExitStack

import concourse.mybir as mybir
from concourse.masks import make_identity

K, T, S, H, T2, J, N = 1024, 2048, 1024, 1024, 2048, 1024, 512
FLOPS = 2 * K * H * S + 2 * H * N * J

F32 = mybir.dt.float32
BF16 = mybir.dt.bfloat16
I32 = mybir.dt.int32
U32 = mybir.dt.uint32
U16 = mybir.dt.uint16
U8 = mybir.dt.uint8
E4M3X4 = mybir.dt.float8_e4m3fn_x4
E2M1X4 = mybir.dt.float4_e2m1fn_x4
ADD = mybir.AluOpType.add
MAX = mybir.AluOpType.max
COPY = mybir.ActivationFunctionType.Copy
RELU = mybir.ActivationFunctionType.Relu

P = 128
PACK = 4
K_PASS = P * PACK
PASSES = 2
BANK = 512
SLICES = PASSES * PACK
SLOTS = 5
CHAIN_PAIR = (0, 0, 1, 2, 2, 0, 1, 3)
SCORE_PAIR = (0, 1, 3, 0)
CHUNK = 256
CHUNKS = J // CHUNK


def tile_list_limb_fall_page_kernel(
    tc, tab_words, tab_scales, offs, w1, page0, offs2, recall, offs3, w2_words, w2_scales, wind, out
):
    nc = tc.nc
    with ExitStack() as ctx:
        held = ctx.enter_context(tc.tile_pool(name="held", bufs=1))
        work = ctx.enter_context(tc.tile_pool(name="work", bufs=2))
        psum = ctx.enter_context(tc.psum_pool(name="psum", bufs=1))

        def bank(k):
            return psum.tile([P, BANK], F32, name="bank%d" % k, tag="bank%d" % k)

        def slot(k, shape=(P, S), dtype=F32):
            return held.tile(list(shape), dtype, name="slot%d" % (k % SLOTS), tag="slot%d" % (k % SLOTS))

        def turned(k, shape, dtype):
            return held.tile(shape, dtype, name="turned%d" % (k % 4), tag="turned%d" % (k % 4), align_bytes=64)

        idx1 = held.tile([P, S // 16], U16, name="idx1")
        idx2 = held.tile([P, S // 16], U16, name="idx2")
        idx3 = held.tile([P, J // 16], U16, name="idx3")
        tab_plane = held.tile([P, T], U8, name="tab_plane", align_bytes=64)
        w2_plane = held.tile([P, PASSES, N], U8, name="w2_plane", align_bytes=64)
        ident = held.tile([P, P], F32, name="ident")
        nc.vector.memset(tab_plane[:].bitcast(I32), 0)
        nc.vector.memset(w2_plane[:].rearrange("p a n -> p (a n)").bitcast(I32), 0)

        page_rows = page0.rearrange("(b p t) c -> b t p c", b=PASSES, t=PACK)
        pages = [held.tile([P, T2], F32, name="page%d" % i) for i in range(SLICES)]
        tab_w = [held.tile([P, T], I32, name="tab_w%d" % a) for a in range(PASSES)]
        w1_raw = {}

        def load_page(i):
            nc.sync.dma_start(pages[i][:], page_rows[i // PACK, i % PACK])

        def load_tab(a):
            nc.sync.dma_start(tab_w[a][:], tab_words[a].rearrange("p t i -> p (t i)").bitcast(I32))

        def load_w1(a, b):
            if (a, b) == (1, 0):
                raw = slot(0, (P, PACK, K_PASS))
            else:
                raw = work.tile([P, PACK, K_PASS], F32, name="w1_raw", tag="stage", bufs=3)
            rows = w1[a * K_PASS : (a + 1) * K_PASS, b * K_PASS : (b + 1) * K_PASS]
            nc.sync.dma_start(raw[:], rows.rearrange("(p j) c -> p j c", j=PACK))
            w1_raw[a, b] = raw

        nc.sync.dma_start(idx1[:], offs)
        rec = held.tile([P, PASSES, PACK], F32, name="rec")
        nc.scalar.dma_start(rec[:], recall.rearrange("(b p t) -> p b t", b=PASSES, t=PACK))
        for q in range(4):
            nc.gpsimd.dma_start(
                tab_plane[32 * q : 32 * q + 4 * PASSES, :].bitcast(I32),
                tab_scales[:, 4 * q : 4 * q + 4, :].bitcast(I32),
            )
        make_identity(nc, ident[:])
        load_tab(0)
        nc.sync.dma_start(idx2[:], offs2)
        load_page(0)
        load_tab(1)
        load_w1(0, 0)
        load_w1(1, 0)
        for i in range(1, 4):
            load_page(i)
        nc.sync.dma_start(idx3[:], offs3)
        load_w1(0, 1)
        load_w1(1, 1)
        for i in range(4, SLICES):
            load_page(i)
        w2_w = held.tile([P, PASSES, 2 * N], U8, name="w2_w", align_bytes=64)
        nc.sync.dma_start(w2_w[:].bitcast(I32), w2_words.rearrange("a p c -> p a c").bitcast(I32))
        for q in range(4):
            nc.sync.dma_start(
                w2_plane[32 * q : 32 * q + 4, :, :].bitcast(I32),
                w2_scales[:, 4 * q : 4 * q + 4, :].rearrange("a r n -> r a n").bitcast(I32),
            )
        winds = []
        for pair in range(2):
            wt = work.tile([P, 2, J], F32, name="wind_t", tag="stage", bufs=3)
            rows = wind[pair * 2 * P : (pair + 1) * 2 * P, :]
            nc.sync.dma_start(wt[:], rows.rearrange("(u p) j -> p u j", u=2))
            winds.append(wt)

        keep = held.tile([P, PASSES, PACK], F32, name="keep")

        v_plane = held.tile([P, S], U8, name="v_plane", align_bytes=64)
        v_w = [held.tile([P, S], U32, name="v_w%d" % a, align_bytes=64) for a in range(PASSES)]
        olds = {}

        def gather_old(i):
            old = slot(i + 1)
            nc.vector.tensor_copy(old[:], pages[i][:].indirect(idx2[:]))
            olds[i] = old

        nc.vector.tensor_copy(v_w[0][:], tab_w[0][:].bitcast(U32).indirect(idx1[:]))
        nc.vector.tensor_copy(v_plane[:], tab_plane[:].indirect(idx1[:]))
        gather_old(0)
        nc.vector.tensor_copy(v_w[1][:], tab_w[1][:].bitcast(U32).indirect(idx1[:]))

        w1_q = {}

        def quantize_w1(a, b, t0, t1, grouped):
            width = (t1 - t0) * P
            nc.scalar.copy(
                grouped[:].rearrange("p (t m j) -> p m t j", m=P, j=PACK),
                w1_raw[a, b][:].rearrange("p j (m t) -> p m t j", t=PACK)[:, :, t0:t1, :],
            )
            codes = held.tile([P, width], U32, name="w1_codes%d%d%d" % (a, b, t0), align_bytes=64)
            plane = held.tile([P, width], U8, name="w1_plane%d%d%d" % (a, b, t0), align_bytes=64)
            nc.vector.quantize_mx(codes[:].bitcast(E4M3X4), plane[:], grouped[:])
            for t in range(t0, t1):
                cols = slice((t - t0) * P, (t - t0 + 1) * P)
                w1_q[a, b, t] = (codes[:, cols], plane[:, cols])

        parts = {}

        def make_parts(i):
            b, t = divmod(i, PACK)
            old = olds[i]
            scratch = slot(i)
            rise_t = turned(i, [P, S], F32)
            rise = work.tile([P, S], F32, name="rise")
            halves = [slice(half * BANK, (half + 1) * BANK) for half in range(2)]
            for half, js in enumerate(halves):
                acc = bank(2 * CHAIN_PAIR[i] + half)
                for a in range(PASSES):
                    codes, plane = w1_q[a, b, t]
                    nc.tensor.matmul_mx(
                        acc[:],
                        lhsT=codes.bitcast(E4M3X4),
                        lhsT_scale=plane,
                        rhs=v_w[a][:, js].bitcast(E4M3X4),
                        rhs_scale=v_plane[4 * a : P, js],
                        start=(a == 0),
                        stop=(a == PASSES - 1),
                    )
                nc.scalar.activation(scratch[:, js], acc[:], COPY, scale=-1.0)
            for half, js in enumerate(halves):
                diff = bank(2 * CHAIN_PAIR[i] + half)
                for q in range(4):
                    blk = slice(q * P, (q + 1) * P)
                    src = slice(half * BANK + q * P, half * BANK + (q + 1) * P)
                    nc.tensor.matmul(diff[:, blk], scratch[:, src], ident[:], start=True, stop=False, is_transpose=True)
                    nc.tensor.matmul(diff[:, blk], old[:, src], ident[:], start=False, stop=True, is_transpose=True)
                nc.scalar.activation(rise_t[:, js], diff[:], RELU, scale=-1.0)
            for half, js in enumerate(halves):
                back = bank(2 * CHAIN_PAIR[i] + half)
                for q in range(4):
                    src = slice(half * BANK + q * P, half * BANK + (q + 1) * P)
                    nc.tensor.transpose(back[:, q * P : (q + 1) * P], rise_t[:, src], ident[:])
                nc.scalar.copy(rise[:, js], back[:])
            nc.scalar.activation(scratch[:], old[:], COPY, scale=keep[:, b, t : t + 1])
            parts[i] = (rise, scratch)

        picked = {}

        def update(i):
            rise, base = parts[i]
            nc.vector.tensor_tensor(pages[i][:].indirect(idx2[:]), rise[:], base[:], ADD)

        def pick(i, tile, j0, c0, c1):
            nc.vector.tensor_copy(
                tile[:, i % PACK, c0 * CHUNK - j0 : c1 * CHUNK - j0],
                pages[i][:].indirect(idx3[:, c0 * CHUNK // 16 : c1 * CHUNK // 16]),
            )
            for c in range(c0, c1):
                picked[i // PACK, c] = (tile, j0)

        x_q = {}

        def quantize_x(b, c0, c1, grouped):
            width = (c1 - c0) * CHUNK
            tile, j0 = picked[b, c0]
            nc.scalar.copy(
                grouped[:].rearrange("p (c i t) -> p c t i", i=4, t=PACK),
                tile[:, :, c0 * CHUNK - j0 : c1 * CHUNK - j0].rearrange("p t (c i) -> p c t i", i=4),
            )
            codes = held.tile([P, width], U32, name="x_codes%d%d" % (b, c0), align_bytes=64)
            plane = held.tile([P, width], U8, name="x_plane%d%d" % (b, c0), align_bytes=64)
            nc.vector.quantize_mx(codes[:].bitcast(E4M3X4), plane[:], grouped[:])
            for c in range(c0, c1):
                cols = slice((c - c0) * CHUNK, (c - c0 + 1) * CHUNK)
                x_q[b, c] = (codes[:, cols], plane[:, cols])

        y_banks = {}

        def score_pass(b, c):
            codes, plane = x_q[b, c]
            for pair in range(2):
                if b == 0:
                    y_banks[c, pair] = bank(2 * SCORE_PAIR[c] + pair)
                acc = y_banks[c, pair]
                for u in range(2):
                    n0 = (2 * pair + u) * P
                    nc.tensor.matmul_mx(
                        acc[:, u * CHUNK : (u + 1) * CHUNK],
                        lhsT=w2_w[:, b, 2 * n0 : 2 * (n0 + P)].bitcast(E2M1X4),
                        lhsT_scale=w2_plane[:, b, n0 : n0 + P],
                        rhs=codes.bitcast(E4M3X4),
                        rhs_scale=plane,
                        start=(b == 0 and u == 0),
                        stop=(b == PASSES - 1 and u == 1),
                    )

        def finish(c):
            js = slice(c * CHUNK, (c + 1) * CHUNK)
            for pair in range(2):
                res = work.tile([P, 2, CHUNK], F32, name="res", bufs=4)
                acc = y_banks[c, pair]
                nc.vector.tensor_tensor(
                    res[:], acc[:].rearrange("p (u j) -> p u j", u=2), winds[pair][:, :, js], MAX
                )
                rows = out[pair * 2 * P : (pair + 1) * 2 * P, js]
                nc.sync.dma_start(rows.rearrange("(u p) j -> p u j", u=2), res[:])

        nc.scalar.activation(keep[:], rec[:], COPY, bias=1.0)
        for a, t0, t1 in ((0, 0, PACK), (1, 0, 1), (1, 1, PACK)):
            grouped = held.tile([P, PACK * (t1 - t0) * P], BF16, name="w1_grouped%d%d" % (a, t0), align_bytes=64)
            quantize_w1(a, 0, t0, t1, grouped)
        make_parts(0)
        for i in range(1, SLOTS - 1):
            gather_old(i)
        first = held.tile([P, PACK, J], BF16, name="first")
        early = held.tile([P, PACK, J // 2], BF16, name="early")
        for i in range(SLICES):
            if i + 1 < SLICES:
                make_parts(i + 1)
            update(i)
            if i + SLOTS - 1 < SLICES:
                gather_old(i + SLOTS - 1)
            if i < PACK:
                pick(i, first, 0, 0, CHUNKS)
            elif i < SLICES - 1:
                pick(i, early, 0, 0, CHUNKS // 2)
            if i < PASSES:
                quantize_w1(i, 1, 0, PACK, turned(i, [P, PACK * K_PASS], BF16))
            if i in (4, 5):
                c0 = 2 * (i - 4)
                quantize_x(0, c0, c0 + 2, turned(i, [P, 2 * PACK * CHUNK], BF16))
        for c in range(CHUNKS - 1):
            score_pass(0, c)
        late = slot(SLICES - 1, (P, PACK, J // 2), BF16)
        for c in range(CHUNKS):
            if c < CHUNKS // 2:
                pick(SLICES - 1, early, 0, c, c + 1)
            if c == CHUNKS // 2:
                for i in range(PACK, SLICES):
                    pick(i, late, J // 2, CHUNKS // 2, CHUNKS)
                finish(0)
            grouped = work.tile([P, PACK * CHUNK], BF16, name="x_grouped", bufs=4, align_bytes=64)
            quantize_x(1, c, c + 1, grouped)
            if c == CHUNKS - 1:
                score_pass(0, c)
            score_pass(1, c)
            if c >= CHUNKS // 2:
                finish(c - 1)
        finish(CHUNKS - 1)
